import numpy as np
import ml_dtypes


def mxq(x, axis, fmt="e4m3"):
    dtype, down = {"e4m3": (ml_dtypes.float8_e4m3fn, 7), "e5m2": (ml_dtypes.float8_e5m2, 14)}[fmt]
    v = np.moveaxis(np.asarray(x, np.float32).astype(ml_dtypes.bfloat16).astype(np.float64), axis, -1)
    blocks = v.reshape(v.shape[:-1] + (-1, 32))
    amax = np.abs(blocks).max(-1, keepdims=True)
    byte = np.maximum(np.where(amax > 0, np.frexp(amax)[1] - 1 + 127, 0) - down, 1)
    scale = np.exp2(byte - 127.0)
    codes = (blocks / scale).astype(np.float32).astype(dtype).astype(np.float64)
    return np.moveaxis((codes * scale).reshape(v.shape), -1, axis)


WIDE = False


def mx_kscale(k):
    if not WIDE:
        return np.ones(k)
    levels = np.array([30, -30])
    if k % 512:
        return np.exp2(np.random.permutation(np.resize(levels, k // 32))).repeat(32)
    a = np.empty((k // 512, 16))
    for p in range(k // 512):
        a[p, :8] = np.random.permutation(np.resize(levels, 8))
        for g in range(8):
            far = levels[np.abs(levels - a[p, g]) >= 10]
            a[p, g + 8] = far[np.random.randint(len(far))]
    return np.exp2(a.ravel()).repeat(32)


def f64(x):
    return np.asarray(x).astype(np.float64)


def striped(idx):
    return np.tile(np.asarray(idx).reshape(-1, 16).T, (8, 1)).astype(np.uint16)


def unstriped(offs):
    return offs[:16].T.reshape(-1).astype(np.int64)


E2M1 = np.array([0.0, 0.5, 1.0, 1.5, 2.0, 3.0, 4.0, 6.0, -0.0, -0.5, -1.0, -1.5, -2.0, -3.0, -4.0, -6.0])


def pack_weight(w, fmt):
    k, n = w.shape
    w = f64(np.asarray(w, np.float32).astype(ml_dtypes.bfloat16)).reshape(k // 32, 32, n)
    amax = np.abs(w).max(1)
    if fmt == "e4m3":
        byte = np.frexp(amax)[1] - 1 + 127 - 7
    else:
        mant, ex = np.frexp(amax / 6.0)
        byte = np.where(mant > 0.5, ex, ex - 1) + 127
    byte = np.clip(np.where(amax > 0, byte, 1), 1, 254)
    scaled = (w * np.exp2(127.0 - byte)[:, None, :]).reshape(k, n).astype(np.float32)
    by_word = np.ascontiguousarray(scaled.reshape(k // 512, 128, 4, n).transpose(0, 1, 3, 2))
    if fmt == "e4m3":
        words = by_word.astype(ml_dtypes.float8_e4m3fn).view(np.uint8)
    else:
        c = by_word.astype(ml_dtypes.float4_e2m1fn).view(np.uint8) & 0xF
        words = (c[..., 0::2] | (c[..., 1::2] << 4)).reshape(k // 512, 128, 2 * n)
    return np.ascontiguousarray(words), np.ascontiguousarray(byte.astype(np.uint8).reshape(k // 512, 16, n))


def unpack_weight(words, scales, fmt):
    g, _, n = scales.shape
    words = np.ascontiguousarray(words).reshape(g, 128, n, -1)
    if fmt == "e4m3":
        vals = words.view(ml_dtypes.float8_e4m3fn).astype(np.float64)
    else:
        nib = np.empty((g, 128, n, 4), np.uint8)
        nib[..., 0::2] = words & 0xF
        nib[..., 1::2] = words >> 4
        vals = E2M1[nib]
    vals = vals * np.repeat(np.exp2(scales.astype(np.float64) - 127.0), 8, axis=1)[..., None]
    return vals.transpose(0, 1, 3, 2).reshape(g * 512, n)


K, N, T, J, R = 512, 512, 2048, 512, 128


def setup_inputs():
    n = np.random.standard_normal
    idx = np.random.permutation(T)[:J]
    fj = mx_kscale(J)
    fk = mx_kscale(K)
    tj = np.ones(T)
    tj[idx] = fj
    drp = pack_weight(n((K, R)) * 1 / np.sqrt(K) / fk[:, None], "e4m3")
    return {
        "xt": (n((K, T)) * tj * fk[:, None]).astype(np.float32),
        "g": (n((N, T)) * np.exp(0.5 * n((1, T))) / tj).astype(np.float32),
        "dr_words": drp[0],
        "dr_scales": drp[1],
        "old": (1.0 * n((R, N))).astype(np.float32),
        "offs": striped(idx),
    }


def reference(xt, g, dr_words, dr_scales, old, offs):
    idx = unstriped(offs)
    dru = unpack_weight(dr_words, dr_scales, "e4m3")
    xj = f64(xt)[:, idx].T
    gj = f64(g)[:, idx].T
    xjq = mxq(xj, 0, "e4m3")
    gjq = mxq(gj, 0, "e5m2")
    w = xjq.T @ gjq
    wq = mxq(w, 0, "e4m3")
    v = dru.T @ wq
    y = 0.04 * v + 0.5 * f64(old)
    return y

@@ -1,0 +1,106 @@
+from contextlib import ExitStack
+
+import concourse.mybir as mybir
+from concourse.masks import make_identity
+
+K, N, T, J, R = 512, 512, 2048, 512, 128
+P = 128
+FLOPS = 2 * J * K * N + 2 * K * R * N
+
+F32 = mybir.dt.float32
+BF16 = mybir.dt.bfloat16
+I32 = mybir.dt.int32
+U32 = mybir.dt.uint32
+U16 = mybir.dt.uint16
+U8 = mybir.dt.uint8
+E4M3 = mybir.dt.float8_e4m3fn_x4
+E5M2 = mybir.dt.float8_e5m2_x4
+MULT = mybir.AluOpType.mult
+ADD = mybir.AluOpType.add
+
+
+def tile_moe_expert_wgrad_directions_kernel(tc, xt, g, dr_words, dr_scales, old, offs, out):
+    nc = tc.nc
+    blocks = K // P
+    with ExitStack() as ctx:
+        keep = ctx.enter_context(tc.tile_pool(name="keep", bufs=1))
+        ring = ctx.enter_context(tc.tile_pool(name="ring", bufs=3))
+        psum = ctx.enter_context(tc.psum_pool(name="psum", bufs=1))
+
+        offsets = keep.tile([P, J // 16], U16, name="offsets")
+        x_rows = [keep.tile([P, T], F32, name="x_rows%d" % a) for a in range(blocks)]
+        g_rows = [keep.tile([P, T], F32, name="g_rows%d" % a) for a in range(blocks)]
+        old_sb = keep.tile([P, N], F32, name="old_sb")
+        old_half = keep.tile([P, N], F32, name="old_half")
+        dr_codes = keep.tile([P, R], U32, name="dr_codes", align_bytes=64)
+        dr_plane = keep.tile([P, R], U8, name="dr_plane", align_bytes=64)
+        ident = keep.tile([P, P], F32, name="ident")
+        x_codes = keep.tile([P, K], U32, name="x_codes", align_bytes=64)
+        x_plane = keep.tile([P, K], U8, name="x_plane", align_bytes=64)
+        w_codes = keep.tile([P, N], U32, name="w_codes", align_bytes=64)
+        w_plane = keep.tile([P, N], U8, name="w_plane", align_bytes=64)
+        res = keep.tile([P, N], F32, name="res")
+
+        nc.sync.dma_start(x_rows[0][:], xt[0:P, :])
+        nc.sync.dma_start(offsets[:], offs)
+        for a in range(1, blocks):
+            nc.sync.dma_start(x_rows[a][:], xt[a * P:(a + 1) * P, :])
+        for a in range(blocks):
+            nc.sync.dma_start(g_rows[a][:], g[a * P:(a + 1) * P, :])
+        nc.gpsimd.memset(dr_plane[:].bitcast(I32), 0)
+        make_identity(nc, ident[:])
+        nc.sync.dma_start(old_sb[:], old)
+        nc.sync.dma_start(dr_codes[:].bitcast(I32), dr_words[0].rearrange("p c t -> p (c t)").bitcast(I32))
+        for q in range(4):
+            nc.sync.dma_start(dr_plane[32 * q:32 * q + 4, :].bitcast(I32), dr_scales[0, 4 * q:4 * q + 4, :].bitcast(I32))
+
+        def turn_and_quantise(pairs, tag, nbufs, codes, plane, fmt):
+            words = pairs[:].bitcast(F32)
+            turned = psum.tile([P, 2, P], F32, name="turned", tag=tag, bufs=nbufs)
+            for u in range(2):
+                nc.tensor.transpose(turned[:, u, :], words[:, u * P:(u + 1) * P], ident[:])
+            grouped = ring.tile([P, 4 * P], BF16, name="grouped", align_bytes=64)
+            nc.scalar.copy(grouped[:].bitcast(F32).rearrange("p (c u) -> p c u", u=2), turned[:].rearrange("p u c -> p c u"))
+            nc.vector.quantize_mx(out=codes.bitcast(fmt), scales=plane, in_=grouped[:])
+
+        def gather(rows):
+            picked = ring.tile([P, J], BF16, name="picked", align_bytes=64)
+            nc.vector.tensor_copy(picked[:].rearrange("f (u b i) -> f b u i", u=2, i=16), rows[:].indirect(offsets[:]))
+            return picked
+
+        def finish(cols, tag):
+            width = cols.stop - cols.start
+            v = psum.tile([P, width], F32, name="v", tag=tag, bufs=1)
+            nc.tensor.matmul_mx(out=v[:], lhsT=dr_codes[:].bitcast(E4M3), lhsT_scale=dr_plane[:],
+                                rhs=w_codes[:, cols].bitcast(E4M3), rhs_scale=w_plane[:, cols], start=True, stop=True)
+            nc.vector.scalar_tensor_tensor(res[:, cols], v[:], 0.04, old_half[:, cols], MULT, ADD)
+            nc.sync.dma_start(out[:, cols], res[:, cols])
+
+        for a in range(blocks):
+            cols = slice(a * P, (a + 1) * P)
+            turn_and_quantise(gather(x_rows[a]), "turn_j", 2, x_codes[:, cols], x_plane[:, cols], E4M3)
+
+        def first_half(b):
+            g_codes = ring.tile([P, P], U32, name="g_codes", align_bytes=64)
+            g_plane = ring.tile([P, P], U8, name="g_plane", align_bytes=64)
+            turn_and_quantise(gather(g_rows[b]), "turn_j", 2, g_codes[:], g_plane[:], E5M2)
+            wt = psum.tile([P, K], F32, name="wt", bufs=2)
+            nc.tensor.matmul_mx(out=wt[:], lhsT=g_codes[:].bitcast(E5M2), lhsT_scale=g_plane[:],
+                                rhs=x_codes[:].bitcast(E4M3), rhs_scale=x_plane[:], start=True, stop=True)
+            return wt
+
+        def second_half(b, wt):
+            cols = slice(b * P, (b + 1) * P)
+            wt_pairs = ring.tile([P, K], BF16, name="wt_pairs", align_bytes=64)
+            src = wt[:].rearrange("n (p u e) -> n u p e", u=2, e=2)
+            dst = wt_pairs[:].rearrange("n (u p e) -> n u p e", u=2, e=2)
+            for u in range(2):
+                nc.scalar.copy(dst[:, u], src[:, u])
+            turn_and_quantise(wt_pairs, "turn_k", 1, w_codes[:, cols], w_plane[:, cols], E4M3)
+
+        for b in range(blocks):
+            second_half(b, first_half(b))
+        nc.vector.tensor_scalar(old_half[:], old_sb[:], 0.5, None, MULT)
+        finish(slice(0, 2 * P), "v01")
+        finish(slice(2 * P, 3 * P), "v2")
+        finish(slice(3 * P, 4 * P), "v3")

@@ -29,17 +29,15 @@ def tile_moe_expert_wgrad_directions_kernel(tc, xt, g, dr_words, dr_scales, old,
 
         offsets = keep.tile([P, J // 16], U16, name="offsets")
         x_rows = [keep.tile([P, T], F32, name="x_rows%d" % a) for a in range(blocks)]
-        g_rows = [keep.tile([P, T], F32, name="g_rows%d" % a) for a in range(blocks)]
+        g_rows = [keep.tile([P, T], F32, name="g_rows%d" % a, tag="g_rows%d" % a, align_bytes=64) for a in range(blocks)]
         old_sb = keep.tile([P, N], F32, name="old_sb")
-        old_half = keep.tile([P, N], F32, name="old_half")
         dr_codes = keep.tile([P, R], U32, name="dr_codes", align_bytes=64)
         dr_plane = keep.tile([P, R], U8, name="dr_plane", align_bytes=64)
         ident = keep.tile([P, P], F32, name="ident")
-        x_codes = keep.tile([P, K], U32, name="x_codes", align_bytes=64)
+        x_grouped = keep.tile([P, 4 * K], BF16, name="x_grouped", align_bytes=64)
+        old_half = keep.tile([P, N], F32, name="old_half")
         x_plane = keep.tile([P, K], U8, name="x_plane", align_bytes=64)
-        w_codes = keep.tile([P, N], U32, name="w_codes", align_bytes=64)
         w_plane = keep.tile([P, N], U8, name="w_plane", align_bytes=64)
-        res = keep.tile([P, N], F32, name="res")
 
         nc.sync.dma_start(x_rows[0][:], xt[0:P, :])
         nc.sync.dma_start(offsets[:], offs)
@@ -54,53 +52,79 @@ def tile_moe_expert_wgrad_directions_kernel(tc, xt, g, dr_words, dr_scales, old,
         for q in range(4):
             nc.sync.dma_start(dr_plane[32 * q:32 * q + 4, :].bitcast(I32), dr_scales[0, 4 * q:4 * q + 4, :].bitcast(I32))
 
-        def turn_and_quantise(pairs, tag, nbufs, codes, plane, fmt):
+        def turn(pairs, bank, grouped):
             words = pairs[:].bitcast(F32)
-            turned = psum.tile([P, 2, P], F32, name="turned", tag=tag, bufs=nbufs)
+            turned = psum.tile([P, 2, P], F32, name="turned", tag=bank)
             for u in range(2):
                 nc.tensor.transpose(turned[:, u, :], words[:, u * P:(u + 1) * P], ident[:])
-            grouped = ring.tile([P, 4 * P], BF16, name="grouped", align_bytes=64)
-            nc.scalar.copy(grouped[:].bitcast(F32).rearrange("p (c u) -> p c u", u=2), turned[:].rearrange("p u c -> p c u"))
-            nc.vector.quantize_mx(out=codes.bitcast(fmt), scales=plane, in_=grouped[:])
+            nc.scalar.copy(grouped.bitcast(F32).rearrange("p (c u) -> p c u", u=2), turned[:].rearrange("p u c -> p c u"))
 
         def gather(rows):
             picked = ring.tile([P, J], BF16, name="picked", align_bytes=64)
             nc.vector.tensor_copy(picked[:].rearrange("f (u b i) -> f b u i", u=2, i=16), rows[:].indirect(offsets[:]))
             return picked
 
-        def finish(cols, tag):
-            width = cols.stop - cols.start
-            v = psum.tile([P, width], F32, name="v", tag=tag, bufs=1)
-            nc.tensor.matmul_mx(out=v[:], lhsT=dr_codes[:].bitcast(E4M3), lhsT_scale=dr_plane[:],
-                                rhs=w_codes[:, cols].bitcast(E4M3), rhs_scale=w_plane[:, cols], start=True, stop=True)
-            nc.vector.scalar_tensor_tensor(res[:, cols], v[:], 0.04, old_half[:, cols], MULT, ADD)
-            nc.sync.dma_start(out[:, cols], res[:, cols])
+        def finish(parts, bank, res_tag):
+            first, width = parts[0].start, parts[-1].stop - parts[0].start
+            v = psum.tile([P, width], F32, name="v", tag=bank)
+            for cols in parts:
+                nc.tensor.matmul_mx(out=v[:, cols.start - first:cols.stop - first],
+                                    lhsT=dr_codes[:].bitcast(E4M3), lhsT_scale=dr_plane[:],
+                                    rhs=w_codes[:, cols].bitcast(E4M3), rhs_scale=w_plane[:, cols], start=True, stop=True)
+            res = keep.tile([P, width], F32, name="res", tag=res_tag, align_bytes=64)
+            nc.vector.scalar_tensor_tensor(res[:], v[:], 0.04, old_half[:, first:first + width], MULT, ADD)
+            nc.sync.dma_start(out[:, first:first + width], res[:])
 
-        for a in range(blocks):
-            cols = slice(a * P, (a + 1) * P)
-            turn_and_quantise(gather(x_rows[a]), "turn_j", 2, x_codes[:, cols], x_plane[:, cols], E4M3)
+        def pick_g(b):
+            grouped = keep.tile([P, 4 * P], BF16, name="g_grouped", tag="g_grouped%d" % b, align_bytes=64)
+            turn(gather(g_rows[b]), banks[b % 2], grouped[:])
+            return grouped
 
-        def first_half(b):
-            g_codes = ring.tile([P, P], U32, name="g_codes", align_bytes=64)
+        def weight_gradient(grouped, codes_tag):
+            g_codes = keep.tile([P, P], U32, name="g_codes", tag=codes_tag, align_bytes=64)
             g_plane = ring.tile([P, P], U8, name="g_plane", align_bytes=64)
-            turn_and_quantise(gather(g_rows[b]), "turn_j", 2, g_codes[:], g_plane[:], E5M2)
+            nc.vector.quantize_mx(out=g_codes[:].bitcast(E5M2), scales=g_plane[:], in_=grouped[:])
             wt = psum.tile([P, K], F32, name="wt", bufs=2)
             nc.tensor.matmul_mx(out=wt[:], lhsT=g_codes[:].bitcast(E5M2), lhsT_scale=g_plane[:],
                                 rhs=x_codes[:].bitcast(E4M3), rhs_scale=x_plane[:], start=True, stop=True)
-            return wt
-
-        def second_half(b, wt):
-            cols = slice(b * P, (b + 1) * P)
             wt_pairs = ring.tile([P, K], BF16, name="wt_pairs", align_bytes=64)
             src = wt[:].rearrange("n (p u e) -> n u p e", u=2, e=2)
             dst = wt_pairs[:].rearrange("n (u p e) -> n u p e", u=2, e=2)
             for u in range(2):
                 nc.scalar.copy(dst[:, u], src[:, u])
-            turn_and_quantise(wt_pairs, "turn_k", 1, w_codes[:, cols], w_plane[:, cols], E4M3)
+            return wt_pairs
 
-        for b in range(blocks):
-            second_half(b, first_half(b))
+        def turn_w(b, wt_pairs, bank):
+            grouped = keep.tile([P, 4 * P], BF16, name="w_grouped", tag="w_grouped%d" % b, align_bytes=64)
+            turn(wt_pairs, bank, grouped[:])
+            return grouped
+
+        def quantise_w(b, grouped):
+            cols = slice(b * P, (b + 1) * P)
+            nc.vector.quantize_mx(out=w_codes[:, cols].bitcast(E4M3), scales=w_plane[:, cols], in_=grouped[:])
+
+        banks = ("bank_a", "bank_b")
+        for a in range(blocks):
+            turn(gather(x_rows[a]), banks[a % 2], x_grouped[:, 4 * P * a:4 * P * (a + 1)])
+        gg0 = pick_g(0)
+        x_codes = keep.tile([P, K], U32, name="x_codes", tag="g_rows0", align_bytes=64)
+        nc.vector.quantize_mx(out=x_codes[:].bitcast(E4M3), scales=x_plane[:], in_=x_grouped[:])
+        gg1 = pick_g(1)
+        wp0 = weight_gradient(gg0, "g_rows1")
+        gg2 = pick_g(2)
+        wp1 = weight_gradient(gg1, "g_rows2")
+        wg0 = turn_w(0, wp0, "bank_a")
+        gg3 = pick_g(3)
+        wp2 = weight_gradient(gg2, "g_rows3")
+        w_codes = keep.tile([P, N], U32, name="w_codes", tag="g_grouped2", align_bytes=64)
+        quantise_w(0, wg0)
         nc.vector.tensor_scalar(old_half[:], old_sb[:], 0.5, None, MULT)
-        finish(slice(0, 2 * P), "v01")
-        finish(slice(2 * P, 3 * P), "v2")
-        finish(slice(3 * P, 4 * P), "v3")
+        wp3 = weight_gradient(gg3, "g_codes3")
+        wg1 = turn_w(1, wp1, "bank_b")
+        quantise_w(1, wg1)
+        wg2 = turn_w(2, wp2, "bank_b")
+        wg3 = turn_w(3, wp3, "bank_a")
+        quantise_w(2, wg2)
+        quantise_w(3, wg3)
+        finish([slice(0, 2 * P), slice(2 * P, 3 * P)], "bank_b", "w_grouped3")
+        finish([slice(3 * P, 4 * P)], "bank_c", "res3")

@@ -64,7 +64,7 @@ def tile_moe_expert_wgrad_directions_kernel(tc, xt, g, dr_words, dr_scales, old,
             nc.vector.tensor_copy(picked[:].rearrange("f (u b i) -> f b u i", u=2, i=16), rows[:].indirect(offsets[:]))
             return picked
 
-        def finish(parts, bank, res_tag):
+        def finish(parts, bank, res_tag, queue):
             first, width = parts[0].start, parts[-1].stop - parts[0].start
             v = psum.tile([P, width], F32, name="v", tag=bank)
             for cols in parts:
@@ -73,34 +73,31 @@ def tile_moe_expert_wgrad_directions_kernel(tc, xt, g, dr_words, dr_scales, old,
                                     rhs=w_codes[:, cols].bitcast(E4M3), rhs_scale=w_plane[:, cols], start=True, stop=True)
             res = keep.tile([P, width], F32, name="res", tag=res_tag, align_bytes=64)
             nc.vector.scalar_tensor_tensor(res[:], v[:], 0.04, old_half[:, first:first + width], MULT, ADD)
-            nc.sync.dma_start(out[:, first:first + width], res[:])
+            queue.dma_start(out[:, first:first + width], res[:])
 
         def pick_g(b):
             grouped = keep.tile([P, 4 * P], BF16, name="g_grouped", tag="g_grouped%d" % b, align_bytes=64)
             turn(gather(g_rows[b]), banks[b % 2], grouped[:])
             return grouped
 
-        def weight_gradient(grouped, codes_tag):
+        def product(grouped, codes_tag):
             g_codes = keep.tile([P, P], U32, name="g_codes", tag=codes_tag, align_bytes=64)
             g_plane = ring.tile([P, P], U8, name="g_plane", align_bytes=64)
             nc.vector.quantize_mx(out=g_codes[:].bitcast(E5M2), scales=g_plane[:], in_=grouped[:])
             wt = psum.tile([P, K], F32, name="wt", bufs=2)
             nc.tensor.matmul_mx(out=wt[:], lhsT=g_codes[:].bitcast(E5M2), lhsT_scale=g_plane[:],
                                 rhs=x_codes[:].bitcast(E4M3), rhs_scale=x_plane[:], start=True, stop=True)
-            wt_pairs = ring.tile([P, K], BF16, name="wt_pairs", align_bytes=64)
+            return wt
+
+        def round_w(wt, pairs_tag):
+            wt_pairs = keep.tile([P, K], BF16, name="wt_pairs", tag=pairs_tag, align_bytes=64)
             src = wt[:].rearrange("n (p u e) -> n u p e", u=2, e=2)
             dst = wt_pairs[:].rearrange("n (u p e) -> n u p e", u=2, e=2)
             for u in range(2):
                 nc.scalar.copy(dst[:, u], src[:, u])
             return wt_pairs
 
-        def turn_w(b, wt_pairs, bank):
-            grouped = keep.tile([P, 4 * P], BF16, name="w_grouped", tag="w_grouped%d" % b, align_bytes=64)
-            turn(wt_pairs, bank, grouped[:])
-            return grouped
-
-        def quantise_w(b, grouped):
-            cols = slice(b * P, (b + 1) * P)
+        def quantise_w(cols, grouped):
             nc.vector.quantize_mx(out=w_codes[:, cols].bitcast(E4M3), scales=w_plane[:, cols], in_=grouped[:])
 
         banks = ("bank_a", "bank_b")
@@ -110,21 +107,27 @@ def tile_moe_expert_wgrad_directions_kernel(tc, xt, g, dr_words, dr_scales, old,
         x_codes = keep.tile([P, K], U32, name="x_codes", tag="g_rows0", align_bytes=64)
         nc.vector.quantize_mx(out=x_codes[:].bitcast(E4M3), scales=x_plane[:], in_=x_grouped[:])
         gg1 = pick_g(1)
-        wp0 = weight_gradient(gg0, "g_rows1")
+        wt0 = product(gg0, "g_rows1")
+        wt1 = product(gg1, "g_codes1")
+        wp0 = round_w(wt0, "g_grouped1")
         gg2 = pick_g(2)
-        wp1 = weight_gradient(gg1, "g_rows2")
-        wg0 = turn_w(0, wp0, "bank_a")
+        wp1 = round_w(wt1, "pairs1")
+        wg01 = keep.tile([P, 8 * P], BF16, name="wg01", align_bytes=64)
+        turn(wp0, "bank_c", wg01[:, :4 * P])
+        turn(wp1, "bank_d", wg01[:, 4 * P:])
         gg3 = pick_g(3)
-        wp2 = weight_gradient(gg2, "g_rows3")
+        wt2 = product(gg2, "g_rows3")
         w_codes = keep.tile([P, N], U32, name="w_codes", tag="g_grouped2", align_bytes=64)
-        quantise_w(0, wg0)
+        quantise_w(slice(0, 2 * P), wg01)
         nc.vector.tensor_scalar(old_half[:], old_sb[:], 0.5, None, MULT)
-        wp3 = weight_gradient(gg3, "g_codes3")
-        wg1 = turn_w(1, wp1, "bank_b")
-        quantise_w(1, wg1)
-        wg2 = turn_w(2, wp2, "bank_b")
-        wg3 = turn_w(3, wp3, "bank_a")
-        quantise_w(2, wg2)
-        quantise_w(3, wg3)
-        finish([slice(0, 2 * P), slice(2 * P, 3 * P)], "bank_b", "w_grouped3")
-        finish([slice(3 * P, 4 * P)], "bank_c", "res3")
+        wt3 = product(gg3, "g_codes3")
+        wp2 = round_w(wt2, "g_grouped3")
+        wp3 = round_w(wt3, "pairs3")
+        wg2 = keep.tile([P, 4 * P], BF16, name="wg2", align_bytes=64)
+        wg3 = keep.tile([P, 4 * P], BF16, name="wg3", tag="w_grouped3", align_bytes=64)
+        turn(wp2, "bank_c", wg2[:])
+        turn(wp3, "bank_d", wg3[:])
+        quantise_w(slice(2 * P, 3 * P), wg2)
+        quantise_w(slice(3 * P, 4 * P), wg3)
+        finish([slice(0, 2 * P), slice(2 * P, 3 * P)], "bank_c", "w_grouped3", nc.sync)
+        finish([slice(3 * P, 4 * P)], "bank_e", "res3", nc.scalar)

@@ -52,17 +52,17 @@ def tile_moe_expert_wgrad_directions_kernel(tc, xt, g, dr_words, dr_scales, old,
         for q in range(4):
             nc.sync.dma_start(dr_plane[32 * q:32 * q + 4, :].bitcast(I32), dr_scales[0, 4 * q:4 * q + 4, :].bitcast(I32))
 
-        def turn(pairs, bank, grouped):
-            words = pairs[:].bitcast(F32)
+        def turn(halves, bank, grouped):
             turned = psum.tile([P, 2, P], F32, name="turned", tag=bank)
             for u in range(2):
-                nc.tensor.transpose(turned[:, u, :], words[:, u * P:(u + 1) * P], ident[:])
+                nc.tensor.transpose(turned[:, u, :], halves[u], ident[:])
             nc.scalar.copy(grouped.bitcast(F32).rearrange("p (c u) -> p c u", u=2), turned[:].rearrange("p u c -> p c u"))
 
         def gather(rows):
             picked = ring.tile([P, J], BF16, name="picked", align_bytes=64)
-            nc.vector.tensor_copy(picked[:].rearrange("f (u b i) -> f b u i", u=2, i=16), rows[:].indirect(offsets[:]))
-            return picked
+            nc.vector.tensor_copy(picked[:], rows[:].indirect(offsets[:]))
+            words = picked[:].bitcast(F32)
+            return [words[:, u::2] for u in range(2)]
 
         def finish(parts, bank, res_tag, queue):
             first, width = parts[0].start, parts[-1].stop - parts[0].start
@@ -95,7 +95,8 @@ def tile_moe_expert_wgrad_directions_kernel(tc, xt, g, dr_words, dr_scales, old,
             dst = wt_pairs[:].rearrange("n (u p e) -> n u p e", u=2, e=2)
             for u in range(2):
                 nc.scalar.copy(dst[:, u], src[:, u])
-            return wt_pairs
+            words = wt_pairs[:].bitcast(F32)
+            return [words[:, u * P:(u + 1) * P] for u in range(2)]
 
         def quantise_w(cols, grouped):
             nc.vector.quantize_mx(out=w_codes[:, cols].bitcast(E4M3), scales=w_plane[:, cols], in_=grouped[:])

@@ -5,6 +5,7 @@ from concourse.masks import make_identity
 
 K, N, T, J, R = 512, 512, 2048, 512, 128
 P = 128
+PACK = 4
 FLOPS = 2 * J * K * N + 2 * K * R * N
 
 F32 = mybir.dt.float32
@@ -32,103 +33,106 @@ def tile_moe_expert_wgrad_directions_kernel(tc, xt, g, dr_words, dr_scales, old,
         g_rows = [keep.tile([P, T], F32, name="g_rows%d" % a, tag="g_rows%d" % a, align_bytes=64) for a in range(blocks)]
         old_sb = keep.tile([P, N], F32, name="old_sb")
         dr_codes = keep.tile([P, R], U32, name="dr_codes", align_bytes=64)
-        dr_plane = keep.tile([P, R], U8, name="dr_plane", align_bytes=64)
+        dr_scale_sb = keep.tile([P, R], U8, name="dr_scale_sb", align_bytes=64)
         ident = keep.tile([P, P], F32, name="ident")
-        x_grouped = keep.tile([P, 4 * K], BF16, name="x_grouped", align_bytes=64)
+        x_grouped = keep.tile([P, PACK * K], BF16, name="x_grouped", align_bytes=64)
         old_half = keep.tile([P, N], F32, name="old_half")
-        x_plane = keep.tile([P, K], U8, name="x_plane", align_bytes=64)
-        w_plane = keep.tile([P, N], U8, name="w_plane", align_bytes=64)
+        x_scales = keep.tile([P, K], U8, name="x_scales", align_bytes=64)
+        w_scales = keep.tile([P, N], U8, name="w_scales", align_bytes=64)
 
         nc.sync.dma_start(x_rows[0][:], xt[0:P, :])
         nc.sync.dma_start(offsets[:], offs)
+        nc.gpsimd.memset(dr_scale_sb[:].bitcast(I32), 0)
+        for q in range(4):
+            nc.sync.dma_start(dr_scale_sb[32 * q:32 * q + 4, :].bitcast(I32), dr_scales[0, 4 * q:4 * q + 4, :].bitcast(I32))
         for a in range(1, blocks):
             nc.sync.dma_start(x_rows[a][:], xt[a * P:(a + 1) * P, :])
         for a in range(blocks):
             nc.sync.dma_start(g_rows[a][:], g[a * P:(a + 1) * P, :])
-        nc.gpsimd.memset(dr_plane[:].bitcast(I32), 0)
         make_identity(nc, ident[:])
-        nc.sync.dma_start(old_sb[:], old)
         nc.sync.dma_start(dr_codes[:].bitcast(I32), dr_words[0].rearrange("p c t -> p (c t)").bitcast(I32))
-        for q in range(4):
-            nc.sync.dma_start(dr_plane[32 * q:32 * q + 4, :].bitcast(I32), dr_scales[0, 4 * q:4 * q + 4, :].bitcast(I32))
+        nc.sync.dma_start(old_sb[:], old)
 
-        def turn(halves, bank, grouped):
+        def turn(halves, bank, grouped, copy=nc.scalar.copy):
             turned = psum.tile([P, 2, P], F32, name="turned", tag=bank)
             for u in range(2):
                 nc.tensor.transpose(turned[:, u, :], halves[u], ident[:])
-            nc.scalar.copy(grouped.bitcast(F32).rearrange("p (c u) -> p c u", u=2), turned[:].rearrange("p u c -> p c u"))
+            copy(grouped.bitcast(F32).rearrange("p (c u) -> p c u", u=2), turned[:].rearrange("p u c -> p c u"))
 
         def gather(rows):
             picked = ring.tile([P, J], BF16, name="picked", align_bytes=64)
             nc.vector.tensor_copy(picked[:], rows[:].indirect(offsets[:]))
-            words = picked[:].bitcast(F32)
-            return [words[:, u::2] for u in range(2)]
-
-        def finish(parts, bank, res_tag, queue):
-            first, width = parts[0].start, parts[-1].stop - parts[0].start
-            v = psum.tile([P, width], F32, name="v", tag=bank)
-            for cols in parts:
-                nc.tensor.matmul_mx(out=v[:, cols.start - first:cols.stop - first],
-                                    lhsT=dr_codes[:].bitcast(E4M3), lhsT_scale=dr_plane[:],
-                                    rhs=w_codes[:, cols].bitcast(E4M3), rhs_scale=w_plane[:, cols], start=True, stop=True)
-            res = keep.tile([P, width], F32, name="res", tag=res_tag, align_bytes=64)
-            nc.vector.scalar_tensor_tensor(res[:], v[:], 0.04, old_half[:, first:first + width], MULT, ADD)
-            queue.dma_start(out[:, first:first + width], res[:])
+            pairs = picked[:].bitcast(F32)
+            return [pairs[:, u::2] for u in range(2)]
 
         def pick_g(b):
-            grouped = keep.tile([P, 4 * P], BF16, name="g_grouped", tag="g_grouped%d" % b, align_bytes=64)
-            turn(gather(g_rows[b]), banks[b % 2], grouped[:])
+            grouped = keep.tile([P, PACK * P], BF16, name="g_grouped", tag="g_grouped%d" % b, align_bytes=64)
+            turn(gather(g_rows[b]), gather_banks[b % 2], grouped[:])
             return grouped
 
-        def product(grouped, codes_tag):
+        def first_product(g_grouped, codes_tag):
             g_codes = keep.tile([P, P], U32, name="g_codes", tag=codes_tag, align_bytes=64)
-            g_plane = ring.tile([P, P], U8, name="g_plane", align_bytes=64)
-            nc.vector.quantize_mx(out=g_codes[:].bitcast(E5M2), scales=g_plane[:], in_=grouped[:])
+            g_scales = ring.tile([P, P], U8, name="g_scales", align_bytes=64)
+            nc.vector.quantize_mx(out=g_codes[:].bitcast(E5M2), scales=g_scales[:], in_=g_grouped[:])
             wt = psum.tile([P, K], F32, name="wt", bufs=2)
-            nc.tensor.matmul_mx(out=wt[:], lhsT=g_codes[:].bitcast(E5M2), lhsT_scale=g_plane[:],
-                                rhs=x_codes[:].bitcast(E4M3), rhs_scale=x_plane[:], start=True, stop=True)
+            nc.tensor.matmul_mx(out=wt[:], lhsT=g_codes[:].bitcast(E5M2), lhsT_scale=g_scales[:],
+                                rhs=x_codes[:].bitcast(E4M3), rhs_scale=x_scales[:], start=True, stop=True)
             return wt
 
-        def round_w(wt, pairs_tag):
-            wt_pairs = keep.tile([P, K], BF16, name="wt_pairs", tag=pairs_tag, align_bytes=64)
+        def round_w(wt, rounded_tag):
+            rounded = keep.tile([P, K], BF16, name="rounded", tag=rounded_tag, align_bytes=64)
             src = wt[:].rearrange("n (p u e) -> n u p e", u=2, e=2)
-            dst = wt_pairs[:].rearrange("n (u p e) -> n u p e", u=2, e=2)
+            dst = rounded[:].rearrange("n (u p e) -> n u p e", u=2, e=2)
             for u in range(2):
                 nc.scalar.copy(dst[:, u], src[:, u])
-            words = wt_pairs[:].bitcast(F32)
-            return [words[:, u * P:(u + 1) * P] for u in range(2)]
+            pairs = rounded[:].bitcast(F32)
+            return [pairs[:, u * P:(u + 1) * P] for u in range(2)]
 
-        def quantise_w(cols, grouped):
-            nc.vector.quantize_mx(out=w_codes[:, cols].bitcast(E4M3), scales=w_plane[:, cols], in_=grouped[:])
+        def quantise_w(cols, w_grouped):
+            nc.vector.quantize_mx(out=w_codes[:, cols].bitcast(E4M3), scales=w_scales[:, cols], in_=w_grouped[:])
 
-        banks = ("bank_a", "bank_b")
+        def finish(b, bank, result_tag, queue):
+            cols = slice(b * P, (b + 1) * P)
+            v = psum.tile([P, P], F32, name="v", tag=bank)
+            nc.tensor.matmul_mx(out=v[:], lhsT=dr_codes[:].bitcast(E4M3), lhsT_scale=dr_scale_sb[:],
+                                rhs=w_codes[:, cols].bitcast(E4M3), rhs_scale=w_scales[:, cols], start=True, stop=True)
+            result = keep.tile([P, P], F32, name="result", tag=result_tag, align_bytes=64)
+            nc.vector.scalar_tensor_tensor(result[:], v[:], 0.04, old_half[:, cols], MULT, ADD)
+            queue.dma_start(out[:, cols], result[:])
+
+        gather_banks = ("bank_a", "bank_b")
         for a in range(blocks):
-            turn(gather(x_rows[a]), banks[a % 2], x_grouped[:, 4 * P * a:4 * P * (a + 1)])
-        gg0 = pick_g(0)
+            turn(gather(x_rows[a]), gather_banks[a % 2], x_grouped[:, PACK * P * a:PACK * P * (a + 1)])
+
+        g_grouped0 = pick_g(0)
         x_codes = keep.tile([P, K], U32, name="x_codes", tag="g_rows0", align_bytes=64)
-        nc.vector.quantize_mx(out=x_codes[:].bitcast(E4M3), scales=x_plane[:], in_=x_grouped[:])
-        gg1 = pick_g(1)
-        wt0 = product(gg0, "g_rows1")
-        wt1 = product(gg1, "g_codes1")
-        wp0 = round_w(wt0, "g_grouped1")
-        gg2 = pick_g(2)
-        wp1 = round_w(wt1, "pairs1")
-        wg01 = keep.tile([P, 8 * P], BF16, name="wg01", align_bytes=64)
-        turn(wp0, "bank_c", wg01[:, :4 * P])
-        turn(wp1, "bank_d", wg01[:, 4 * P:])
-        gg3 = pick_g(3)
-        wt2 = product(gg2, "g_rows3")
+        nc.vector.quantize_mx(out=x_codes[:].bitcast(E4M3), scales=x_scales[:], in_=x_grouped[:])
+        g_grouped1 = pick_g(1)
+        wt0 = first_product(g_grouped0, "g_rows1")
+        wt1 = first_product(g_grouped1, "g_codes1")
+        halves0 = round_w(wt0, "g_grouped1")
+        g_grouped2 = pick_g(2)
+        halves1 = round_w(wt1, "rounded1")
+        w_grouped01 = keep.tile([P, 2 * PACK * P], BF16, name="w_grouped01", align_bytes=64)
+        turn(halves0, "bank_c", w_grouped01[:, :PACK * P])
+        turn(halves1, "bank_d", w_grouped01[:, PACK * P:])
+
+        g_grouped3 = pick_g(3)
+        wt2 = first_product(g_grouped2, "g_rows3")
         w_codes = keep.tile([P, N], U32, name="w_codes", tag="g_grouped2", align_bytes=64)
-        quantise_w(slice(0, 2 * P), wg01)
+        quantise_w(slice(0, 2 * P), w_grouped01)
         nc.vector.tensor_scalar(old_half[:], old_sb[:], 0.5, None, MULT)
-        wt3 = product(gg3, "g_codes3")
-        wp2 = round_w(wt2, "g_grouped3")
-        wp3 = round_w(wt3, "pairs3")
-        wg2 = keep.tile([P, 4 * P], BF16, name="wg2", align_bytes=64)
-        wg3 = keep.tile([P, 4 * P], BF16, name="wg3", tag="w_grouped3", align_bytes=64)
-        turn(wp2, "bank_c", wg2[:])
-        turn(wp3, "bank_d", wg3[:])
-        quantise_w(slice(2 * P, 3 * P), wg2)
-        quantise_w(slice(3 * P, 4 * P), wg3)
-        finish([slice(0, 2 * P), slice(2 * P, 3 * P)], "bank_c", "w_grouped3", nc.sync)
-        finish([slice(3 * P, 4 * P)], "bank_e", "res3", nc.scalar)
+        wt3 = first_product(g_grouped3, "g_codes3")
+
+        finish(0, "bank_a", "result0", nc.sync)
+        finish(1, "bank_f", "result1", nc.sync)
+        halves2 = round_w(wt2, "g_grouped3")
+        halves3 = round_w(wt3, "rounded3")
+        w_grouped2 = keep.tile([P, PACK * P], BF16, name="w_grouped2", align_bytes=64)
+        w_grouped3 = keep.tile([P, PACK * P], BF16, name="w_grouped3", tag="w_grouped3", align_bytes=64)
+        turn(halves2, "bank_a", w_grouped2[:], nc.vector.tensor_copy)
+        turn(halves3, "bank_f", w_grouped3[:])
+        quantise_w(slice(2 * P, 3 * P), w_grouped2)
+        quantise_w(slice(3 * P, 4 * P), w_grouped3)
+        finish(2, "bank_c", "w_grouped3", nc.sync)
+        finish(3, "bank_e", "result3", nc.scalar)

from contextlib import ExitStack

import concourse.mybir as mybir
from concourse.masks import make_identity

K, N, T, J, R = 512, 512, 2048, 512, 128
P = 128
PACK = 4
FLOPS = 2 * J * K * N + 2 * K * R * N

F32 = mybir.dt.float32
BF16 = mybir.dt.bfloat16
I32 = mybir.dt.int32
U32 = mybir.dt.uint32
U16 = mybir.dt.uint16
U8 = mybir.dt.uint8
E4M3 = mybir.dt.float8_e4m3fn_x4
E5M2 = mybir.dt.float8_e5m2_x4
MULT = mybir.AluOpType.mult
ADD = mybir.AluOpType.add


def tile_moe_expert_wgrad_directions_kernel(tc, xt, g, dr_words, dr_scales, old, offs, out):
    nc = tc.nc
    blocks = K // P
    with ExitStack() as ctx:
        keep = ctx.enter_context(tc.tile_pool(name="keep", bufs=1))
        ring = ctx.enter_context(tc.tile_pool(name="ring", bufs=3))
        psum = ctx.enter_context(tc.psum_pool(name="psum", bufs=1))

        offsets = keep.tile([P, J // 16], U16, name="offsets")
        x_rows = [keep.tile([P, T], F32, name="x_rows%d" % a) for a in range(blocks)]
        g_rows = [keep.tile([P, T], F32, name="g_rows%d" % a, tag="g_rows%d" % a, align_bytes=64) for a in range(blocks)]
        old_sb = keep.tile([P, N], F32, name="old_sb")
        dr_codes = keep.tile([P, R], U32, name="dr_codes", align_bytes=64)
        dr_scale_sb = keep.tile([P, R], U8, name="dr_scale_sb", align_bytes=64)
        ident = keep.tile([P, P], F32, name="ident")
        x_grouped = keep.tile([P, PACK * K], BF16, name="x_grouped", align_bytes=64)
        old_half = keep.tile([P, N], F32, name="old_half")
        x_scales = keep.tile([P, K], U8, name="x_scales", align_bytes=64)
        w_scales = keep.tile([P, N], U8, name="w_scales", align_bytes=64)

        nc.sync.dma_start(x_rows[0][:], xt[0:P, :])
        nc.sync.dma_start(offsets[:], offs)
        nc.gpsimd.memset(dr_scale_sb[:].bitcast(I32), 0)
        for q in range(4):
            nc.sync.dma_start(dr_scale_sb[32 * q:32 * q + 4, :].bitcast(I32), dr_scales[0, 4 * q:4 * q + 4, :].bitcast(I32))
        for a in range(1, blocks):
            nc.sync.dma_start(x_rows[a][:], xt[a * P:(a + 1) * P, :])
        for a in range(blocks):
            nc.sync.dma_start(g_rows[a][:], g[a * P:(a + 1) * P, :])
        make_identity(nc, ident[:])
        nc.sync.dma_start(dr_codes[:].bitcast(I32), dr_words[0].rearrange("p c t -> p (c t)").bitcast(I32))
        nc.sync.dma_start(old_sb[:], old)

        def turn(halves, bank, grouped, copy=nc.scalar.copy):
            turned = psum.tile([P, 2, P], F32, name="turned", tag=bank)
            for u in range(2):
                nc.tensor.transpose(turned[:, u, :], halves[u], ident[:])
            copy(grouped.bitcast(F32).rearrange("p (c u) -> p c u", u=2), turned[:].rearrange("p u c -> p c u"))

        def gather(rows):
            picked = ring.tile([P, J], BF16, name="picked", align_bytes=64)
            nc.vector.tensor_copy(picked[:], rows[:].indirect(offsets[:]))
            pairs = picked[:].bitcast(F32)
            return [pairs[:, u::2] for u in range(2)]

        def pick_g(b):
            grouped = keep.tile([P, PACK * P], BF16, name="g_grouped", tag="g_grouped%d" % b, align_bytes=64)
            turn(gather(g_rows[b]), gather_banks[b % 2], grouped[:])
            return grouped

        def first_product(g_grouped, codes_tag):
            g_codes = keep.tile([P, P], U32, name="g_codes", tag=codes_tag, align_bytes=64)
            g_scales = ring.tile([P, P], U8, name="g_scales", align_bytes=64)
            nc.vector.quantize_mx(out=g_codes[:].bitcast(E5M2), scales=g_scales[:], in_=g_grouped[:])
            wt = psum.tile([P, K], F32, name="wt", bufs=2)
            nc.tensor.matmul_mx(out=wt[:], lhsT=g_codes[:].bitcast(E5M2), lhsT_scale=g_scales[:],
                                rhs=x_codes[:].bitcast(E4M3), rhs_scale=x_scales[:], start=True, stop=True)
            return wt

        def round_w(wt, rounded_tag):
            rounded = keep.tile([P, K], BF16, name="rounded", tag=rounded_tag, align_bytes=64)
            src = wt[:].rearrange("n (p u e) -> n u p e", u=2, e=2)
            dst = rounded[:].rearrange("n (u p e) -> n u p e", u=2, e=2)
            for u in range(2):
                nc.scalar.copy(dst[:, u], src[:, u])
            pairs = rounded[:].bitcast(F32)
            return [pairs[:, u * P:(u + 1) * P] for u in range(2)]

        def quantise_w(cols, w_grouped):
            nc.vector.quantize_mx(out=w_codes[:, cols].bitcast(E4M3), scales=w_scales[:, cols], in_=w_grouped[:])

        def finish(b, bank, result_tag, queue):
            cols = slice(b * P, (b + 1) * P)
            v = psum.tile([P, P], F32, name="v", tag=bank)
            nc.tensor.matmul_mx(out=v[:], lhsT=dr_codes[:].bitcast(E4M3), lhsT_scale=dr_scale_sb[:],
                                rhs=w_codes[:, cols].bitcast(E4M3), rhs_scale=w_scales[:, cols], start=True, stop=True)
            result = keep.tile([P, P], F32, name="result", tag=result_tag, align_bytes=64)
            nc.vector.scalar_tensor_tensor(result[:], v[:], 0.04, old_half[:, cols], MULT, ADD)
            queue.dma_start(out[:, cols], result[:])

        gather_banks = ("bank_a", "bank_b")
        for a in range(blocks):
            turn(gather(x_rows[a]), gather_banks[a % 2], x_grouped[:, PACK * P * a:PACK * P * (a + 1)])

        g_grouped0 = pick_g(0)
        x_codes = keep.tile([P, K], U32, name="x_codes", tag="g_rows0", align_bytes=64)
        nc.vector.quantize_mx(out=x_codes[:].bitcast(E4M3), scales=x_scales[:], in_=x_grouped[:])
        g_grouped1 = pick_g(1)
        wt0 = first_product(g_grouped0, "g_rows1")
        wt1 = first_product(g_grouped1, "g_codes1")
        halves0 = round_w(wt0, "g_grouped1")
        g_grouped2 = pick_g(2)
        halves1 = round_w(wt1, "rounded1")
        w_grouped01 = keep.tile([P, 2 * PACK * P], BF16, name="w_grouped01", align_bytes=64)
        turn(halves0, "bank_c", w_grouped01[:, :PACK * P])
        turn(halves1, "bank_d", w_grouped01[:, PACK * P:])

        g_grouped3 = pick_g(3)
        wt2 = first_product(g_grouped2, "g_rows3")
        w_codes = keep.tile([P, N], U32, name="w_codes", tag="g_grouped2", align_bytes=64)
        quantise_w(slice(0, 2 * P), w_grouped01)
        nc.vector.tensor_scalar(old_half[:], old_sb[:], 0.5, None, MULT)
        wt3 = first_product(g_grouped3, "g_codes3")

        finish(0, "bank_a", "result0", nc.sync)
        finish(1, "bank_f", "result1", nc.sync)
        halves2 = round_w(wt2, "g_grouped3")
        halves3 = round_w(wt3, "rounded3")
        w_grouped2 = keep.tile([P, PACK * P], BF16, name="w_grouped2", align_bytes=64)
        w_grouped3 = keep.tile([P, PACK * P], BF16, name="w_grouped3", tag="w_grouped3", align_bytes=64)
        turn(halves2, "bank_a", w_grouped2[:], nc.vector.tensor_copy)
        turn(halves3, "bank_f", w_grouped3[:])
        quantise_w(slice(2 * P, 3 * P), w_grouped2)
        quantise_w(slice(3 * P, 4 * P), w_grouped3)
        finish(2, "bank_c", "w_grouped3", nc.sync)
        finish(3, "bank_e", "result3", nc.scalar)
